import numpy as np
import ml_dtypes


def mxq(x, axis, fmt="e4m3"):
    dtype, down = {"e4m3": (ml_dtypes.float8_e4m3fn, 7), "e5m2": (ml_dtypes.float8_e5m2, 14)}[fmt]
    v = np.moveaxis(np.asarray(x, np.float32).astype(ml_dtypes.bfloat16).astype(np.float64), axis, -1)
    blocks = v.reshape(v.shape[:-1] + (-1, 32))
    amax = np.abs(blocks).max(-1, keepdims=True)
    byte = np.maximum(np.where(amax > 0, np.frexp(amax)[1] - 1 + 127, 0) - down, 1)
    scale = np.exp2(byte - 127.0)
    codes = (blocks / scale).astype(np.float32).astype(dtype).astype(np.float64)
    return np.moveaxis((codes * scale).reshape(v.shape), -1, axis)


WIDE = False


def mx_kscale(k):
    if not WIDE:
        return np.ones(k)
    levels = np.array([10, -10, 5, -5, 0])
    if k % 512:
        return np.exp2(np.random.permutation(np.resize(levels, k // 32))).repeat(32)
    a = np.empty((k // 512, 16))
    for p in range(k // 512):
        a[p, :8] = np.random.permutation(np.resize(levels, 8))
        for g in range(8):
            far = levels[np.abs(levels - a[p, g]) >= 10]
            a[p, g + 8] = far[np.random.randint(len(far))]
    return np.exp2(a.ravel()).repeat(32)


def f64(x):
    return np.asarray(x).astype(np.float64)


def striped8(idx):
    return np.asarray(idx).reshape(8, -1, 16).transpose(0, 2, 1).reshape(128, -1).astype(np.uint16)


def unstriped8(offs):
    return offs.reshape(8, 16, -1).transpose(0, 2, 1).reshape(8, -1).astype(np.int64)


def pick8(x, idx, run):
    r = np.arange(len(x))
    return x[r[:, None], idx[r % (8 * run) // run]]


E2M1 = np.array([0.0, 0.5, 1.0, 1.5, 2.0, 3.0, 4.0, 6.0, -0.0, -0.5, -1.0, -1.5, -2.0, -3.0, -4.0, -6.0])


def pack_weight(w, fmt):
    k, n = w.shape
    w = f64(np.asarray(w, np.float32).astype(ml_dtypes.bfloat16)).reshape(k // 32, 32, n)
    amax = np.abs(w).max(1)
    if fmt == "e4m3":
        byte = np.frexp(amax)[1] - 1 + 127 - 7
    else:
        mant, ex = np.frexp(amax / 6.0)
        byte = np.where(mant > 0.5, ex, ex - 1) + 127
    byte = np.clip(np.where(amax > 0, byte, 1), 1, 254)
    scaled = (w * np.exp2(127.0 - byte)[:, None, :]).reshape(k, n).astype(np.float32)
    by_word = np.ascontiguousarray(scaled.reshape(k // 512, 128, 4, n).transpose(0, 1, 3, 2))
    if fmt == "e4m3":
        words = by_word.astype(ml_dtypes.float8_e4m3fn).view(np.uint8)
    else:
        c = by_word.astype(ml_dtypes.float4_e2m1fn).view(np.uint8) & 0xF
        words = (c[..., 0::2] | (c[..., 1::2] << 4)).reshape(k // 512, 128, 2 * n)
    return np.ascontiguousarray(words), np.ascontiguousarray(byte.astype(np.uint8).reshape(k // 512, 16, n))


def unpack_weight(words, scales, fmt):
    g, _, n = scales.shape
    words = np.ascontiguousarray(words).reshape(g, 128, n, -1)
    if fmt == "e4m3":
        vals = words.view(ml_dtypes.float8_e4m3fn).astype(np.float64)
    else:
        nib = np.empty((g, 128, n, 4), np.uint8)
        nib[..., 0::2] = words & 0xF
        nib[..., 1::2] = words >> 4
        vals = E2M1[nib]
    vals = vals * np.repeat(np.exp2(scales.astype(np.float64) - 127.0), 8, axis=1)[..., None]
    return vals.transpose(0, 1, 3, 2).reshape(g * 512, n)


D, K, T, I, Q = 512, 512, 1024, 512, 128


def setup_inputs():
    n = np.random.standard_normal
    idx = np.stack([np.random.permutation(T)[:I] for _ in range(8)])
    idx2 = np.stack([np.random.permutation(T)[:I] for _ in range(8)])
    idx3 = np.stack([np.random.permutation(T)[:I] for _ in range(8)])
    idx4 = np.stack([np.random.permutation(T)[:I] for _ in range(8)])
    idx5 = np.stack([np.random.permutation(T)[:I] for _ in range(8)])
    idx6 = np.stack([np.random.permutation(T)[:I] for _ in range(8)])
    fd = mx_kscale(D)
    fk = mx_kscale(K)
    wqp = pack_weight(n((D, K)) * 1.0 / np.sqrt(D) * fd[:, None] * fk, "e4m3")
    keysp = pack_weight(n((K, T)) * 1.0 / np.sqrt(K) / fk[:, None], "e2m1")
    tagsp = pack_weight(n((D, T)) * 0.5 / np.sqrt(D) * fd[:, None], "e4m3")
    return {
        "states": (n((D, Q)) * 0.95 / fd[:, None]).astype(np.float32),
        "wq_words": wqp[0],
        "wq_scales": wqp[1],
        "keys_words": keysp[0],
        "keys_scales": keysp[1],
        "tags_words": tagsp[0],
        "tags_scales": tagsp[1],
        "offs": striped8(idx),
        "offs2": striped8(idx2),
        "offs3": striped8(idx3),
        "offs4": striped8(idx4),
        "offs5": striped8(idx5),
        "offs6": striped8(idx6),
    }


def reference(states, wq_words, wq_scales, keys_words, keys_scales, tags_words, tags_scales, offs, offs2, offs3, offs4, offs5, offs6):
    idx = unstriped8(offs)
    idx2 = unstriped8(offs2)
    idx3 = unstriped8(offs3)
    idx4 = unstriped8(offs4)
    idx5 = unstriped8(offs5)
    idx6 = unstriped8(offs6)
    wqu = unpack_weight(wq_words, wq_scales, "e4m3")
    keysu = unpack_weight(keys_words, keys_scales, "e2m1")
    tagsu = unpack_weight(tags_words, tags_scales, "e4m3")
    statesq = mxq(f64(states), 0, "e4m3")
    qv = wqu.T @ statesq
    qvq = mxq(qv, 0, "e4m3")
    a = qvq.T @ keysu + statesq.T @ tagsu
    f1 = np.zeros((Q, T))
    f1[np.arange(Q)[:, None], idx3[np.arange(Q) % 128 // 16]] = pick8(a, idx, 16)
    f2 = np.zeros((Q, T))
    f2[np.arange(Q)[:, None], idx4[np.arange(Q) % 128 // 16]] = pick8(a, idx2, 16)
    r = np.maximum(f1, f2)
    cc = a + r
    y = pick8(cc, idx5, 16) - pick8(cc, idx6, 16)
    return y

@@ -1,0 +1,174 @@
+from contextlib import ExitStack
+
+import concourse.mybir as mybir
+
+D, K, T, I, Q = 512, 512, 1024, 512, 128
+FLOPS = 2 * Q * (D * K + K * T + D * T)
+
+F32 = mybir.dt.float32
+BF16 = mybir.dt.bfloat16
+I32 = mybir.dt.int32
+U32 = mybir.dt.uint32
+U16 = mybir.dt.uint16
+U8 = mybir.dt.uint8
+FP8X4 = mybir.dt.float8_e4m3fn_x4
+FP4X4 = mybir.dt.float4_e2m1fn_x4
+COPY = mybir.ActivationFunctionType.Copy
+ALU = mybir.AluOpType
+
+P = 128
+PACK = 4
+N_SCORE = 256
+HALF = I // 2
+COLS = HALF // 16
+
+
+def load_scales_all(queue, plane, rows):
+    for quad in range(4):
+        src = rows[0, 4 * quad : 4 * quad + 4, :].bitcast(I32)
+        queue.dma_start(
+            out=plane[32 * quad : 32 * quad + 32, :].bitcast(I32),
+            in_=src.unsqueeze(0).to_broadcast([8, 4, src.shape[1]]),
+        )
+
+
+def load_scales(queue, plane, rows, quads=range(4)):
+    for quad in quads:
+        queue.dma_start(
+            out=plane[32 * quad : 32 * quad + 4, :].bitcast(I32),
+            in_=rows[0, 4 * quad : 4 * quad + 4, :].bitcast(I32),
+        )
+
+
+def tile_attend_passedtwo_madeparts_kernel(
+    tc, states, wq_words, wq_scales, keys_words, keys_scales, tags_words, tags_scales,
+    offs, offs2, offs3, offs4, offs5, offs6, out,
+):
+    nc = tc.nc
+    with ExitStack() as ctx:
+        sb = ctx.enter_context(tc.tile_pool(name="sb", bufs=1))
+        ps = ctx.enter_context(tc.psum_pool(name="ps", bufs=1))
+
+        lists = [sb.tile([P, I // 16], U16, name="list%d" % n) for n in range(6)]
+        wq_raw_sc = sb.tile([P, K], U8, align_bytes=64)
+        keys_sc = sb.tile([P, T], U8, align_bytes=64)
+        tags_sc = sb.tile([P, T], U8, align_bytes=64)
+        st_raw = sb.tile([P, PACK, Q], F32, align_bytes=64)
+        wq_raw = sb.tile([P, K], U32, align_bytes=64)
+        keys_w = sb.tile([P, 2 * T], U8, align_bytes=64)
+        tags_w = sb.tile([P, T], U32, align_bytes=64)
+        f1 = sb.tile([P, T], F32, align_bytes=64)
+        f2 = sb.tile([P, T], F32, align_bytes=64)
+
+
+        nc.sync.dma_start(out=st_raw[:], in_=states.rearrange("(p j) q -> p j q", j=PACK))
+        nc.sync.dma_start(
+            out=wq_raw[:].bitcast(I32), in_=wq_words[0].rearrange("p n t -> p (n t)").bitcast(I32)
+        )
+        load_scales_all(nc.sync, wq_raw_sc, wq_scales)
+        load_scales(nc.gpsimd, tags_sc, tags_scales, (2, 3))
+        load_scales(nc.sync, tags_sc, tags_scales, (0,))
+        nc.sync.dma_start(
+            out=tags_w[:].bitcast(I32), in_=tags_words[0].rearrange("p n t -> p (n t)").bitcast(I32)
+        )
+        load_scales(nc.sync, tags_sc, tags_scales, (1,))
+        nc.sync.dma_start(out=keys_w[:].bitcast(I32), in_=keys_words[0].bitcast(I32))
+        load_scales(nc.sync, keys_sc, keys_scales)
+        for tile, src in zip(lists, (offs, offs2, offs3, offs4, offs5, offs6)):
+            nc.sync.dma_start(tile[:], src)
+
+        nc.vector.memset(f1[:], 0.0)
+        nc.vector.memset(f2[:], 0.0)
+
+        st_bf = sb.tile([P, Q, PACK], BF16, align_bytes=64)
+        nc.scalar.activation(
+            st_bf[:, Q // 2 :, :], st_raw[:, :, Q // 2 :].rearrange("p j q -> p q j"), COPY
+        )
+        nc.vector.tensor_copy(
+            out=st_bf[:, : Q // 2, :], in_=st_raw[:, :, : Q // 2].rearrange("p j q -> p q j")
+        )
+        wq_w = sb.tile([P, K], U32, align_bytes=64)
+        wq_sc = sb.tile([P, K], U8, align_bytes=64)
+        nc.scalar.copy(
+            out=wq_w[:].rearrange("p (t m) -> p m t", t=PACK),
+            in_=wq_raw[:].rearrange("p (m t) -> p m t", t=PACK),
+        )
+        nc.vector.tensor_copy(
+            out=wq_sc[:].rearrange("p (t m) -> p t m", t=PACK),
+            in_=wq_raw_sc[:].rearrange("p (m t) -> p t m", t=PACK),
+        )
+        st_w = sb.tile([P, Q], U32, align_bytes=64)
+        st_sc = sb.tile([P, Q], U8, align_bytes=64)
+        nc.vector.quantize_mx(
+            out=st_w[:].bitcast(FP8X4), scales=st_sc[:], in_=st_bf[:].rearrange("p q j -> p (q j)")
+        )
+
+        qv_ps = ps.tile([P, PACK, Q], F32)
+        for t in range(PACK):
+            cols = slice(t * P, (t + 1) * P)
+            nc.tensor.matmul_mx(
+                out=qv_ps[:, t, :],
+                lhsT=wq_w[:, cols].bitcast(FP8X4), lhsT_scale=wq_sc[:, cols],
+                rhs=st_w[:].bitcast(FP8X4), rhs_scale=st_sc[:],
+                start=True, stop=True,
+            )
+        banks = [ps.tile([P, N_SCORE], F32, name="score%d" % b) for b in range(T // N_SCORE)]
+        for b, bank in enumerate(banks):
+            cols = slice(b * N_SCORE, (b + 1) * N_SCORE)
+            nc.tensor.matmul_mx(
+                out=bank[:],
+                lhsT=st_w[:].bitcast(FP8X4), lhsT_scale=st_sc[:],
+                rhs=tags_w[:, cols].bitcast(FP8X4), rhs_scale=tags_sc[:, cols],
+                start=True, stop=False,
+            )
+
+        qv_bf = sb.tile([P, Q, PACK], BF16, align_bytes=64)
+        nc.scalar.copy(out=qv_bf[:], in_=qv_ps[:].rearrange("p t q -> p q t"))
+        qv_w = sb.tile([P, Q], U32, align_bytes=64)
+        qv_sc = sb.tile([P, Q], U8, align_bytes=64)
+        nc.vector.quantize_mx(
+            out=qv_w[:].bitcast(FP8X4), scales=qv_sc[:], in_=qv_bf[:].rearrange("p q t -> p (q t)")
+        )
+
+        a = sb.tile([P, T], F32, align_bytes=64)
+        for b, bank in enumerate(banks):
+            cols = slice(b * N_SCORE, (b + 1) * N_SCORE)
+            nc.tensor.matmul_mx(
+                out=bank[:],
+                lhsT=qv_w[:].bitcast(FP8X4), lhsT_scale=qv_sc[:],
+                rhs=keys_w[:, 2 * cols.start : 2 * cols.stop].bitcast(FP4X4), rhs_scale=keys_sc[:, cols],
+                start=False, stop=True,
+            )
+            if b % 2 == 0:
+                nc.scalar.copy(out=a[:, cols], in_=bank[:])
+            else:
+                nc.vector.tensor_copy(out=a[:, cols], in_=bank[:])
+
+        g1 = sb.tile([P, I], F32, align_bytes=64)
+        g2 = sb.tile([P, I], F32, align_bytes=64)
+        nc.vector.tensor_copy(g1[:, :HALF], a[:].indirect(lists[0][:, :COLS]))
+        nc.scalar.activation(g1[:, HALF:], a[:].indirect(lists[0][:, COLS:]), COPY)
+        nc.scalar.activation(g2[:], a[:].indirect(lists[1][:]), COPY)
+        nc.vector.tensor_copy(f1[:].indirect(lists[2][:]), g1[:])
+        nc.vector.tensor_copy(f2[:].indirect(lists[3][:]), g2[:])
+
+        r = sb.tile([P, T], F32, align_bytes=64)
+        cc = sb.tile([P, T], F32, align_bytes=64)
+        halves = [slice(h * T // 2, (h + 1) * T // 2) for h in range(2)]
+        for cols in halves:
+            nc.vector.tensor_tensor(r[:, cols], f1[:, cols], f2[:, cols], ALU.max)
+        for cols in halves:
+            nc.vector.tensor_tensor(cc[:, cols], r[:, cols], a[:, cols], ALU.add)
+
+        y5 = sb.tile([P, I], F32, align_bytes=64)
+        y6 = sb.tile([P, I], F32, align_bytes=64)
+        y = sb.tile([P, I], F32, align_bytes=64)
+        for h in range(2):
+            cols = slice(h * HALF, (h + 1) * HALF)
+            lc = slice(h * COLS, (h + 1) * COLS)
+            nc.vector.tensor_copy(y5[:, cols], cc[:].indirect(lists[4][:, lc]))
+            nc.scalar.activation(y6[:, cols], cc[:].indirect(lists[5][:, lc]), COPY)
+        for h in range(2):
+            cols = slice(h * HALF, (h + 1) * HALF)
+            nc.vector.tensor_tensor(y[:, cols], y5[:, cols], y6[:, cols], ALU.subtract)
+            nc.sync.dma_start(out=out[:, cols], in_=y[:, cols])

@@ -57,28 +57,24 @@ def tile_attend_passedtwo_madeparts_kernel(
         wq_raw = sb.tile([P, K], U32, align_bytes=64)
         keys_w = sb.tile([P, 2 * T], U8, align_bytes=64)
         tags_w = sb.tile([P, T], U32, align_bytes=64)
-        f1 = sb.tile([P, T], F32, align_bytes=64)
-        f2 = sb.tile([P, T], F32, align_bytes=64)
 
 
         nc.sync.dma_start(out=st_raw[:], in_=states.rearrange("(p j) q -> p j q", j=PACK))
+        load_scales_all(nc.sync, wq_raw_sc, wq_scales)
         nc.sync.dma_start(
             out=wq_raw[:].bitcast(I32), in_=wq_words[0].rearrange("p n t -> p (n t)").bitcast(I32)
         )
-        load_scales_all(nc.sync, wq_raw_sc, wq_scales)
-        load_scales(nc.gpsimd, tags_sc, tags_scales, (2, 3))
+        load_scales(nc.gpsimd, keys_sc, keys_scales, (3,))
         load_scales(nc.sync, tags_sc, tags_scales, (0,))
         nc.sync.dma_start(
             out=tags_w[:].bitcast(I32), in_=tags_words[0].rearrange("p n t -> p (n t)").bitcast(I32)
         )
-        load_scales(nc.sync, tags_sc, tags_scales, (1,))
+        load_scales(nc.sync, tags_sc, tags_scales, (1, 2, 3))
         nc.sync.dma_start(out=keys_w[:].bitcast(I32), in_=keys_words[0].bitcast(I32))
-        load_scales(nc.sync, keys_sc, keys_scales)
+        load_scales(nc.sync, keys_sc, keys_scales, (0, 1, 2))
         for tile, src in zip(lists, (offs, offs2, offs3, offs4, offs5, offs6)):
             nc.sync.dma_start(tile[:], src)
 
-        nc.vector.memset(f1[:], 0.0)
-        nc.vector.memset(f2[:], 0.0)
 
         st_bf = sb.tile([P, Q, PACK], BF16, align_bytes=64)
         nc.scalar.activation(
@@ -89,10 +85,6 @@ def tile_attend_passedtwo_madeparts_kernel(
         )
         wq_w = sb.tile([P, K], U32, align_bytes=64)
         wq_sc = sb.tile([P, K], U8, align_bytes=64)
-        nc.scalar.copy(
-            out=wq_w[:].rearrange("p (t m) -> p m t", t=PACK),
-            in_=wq_raw[:].rearrange("p (m t) -> p m t", t=PACK),
-        )
         nc.vector.tensor_copy(
             out=wq_sc[:].rearrange("p (t m) -> p t m", t=PACK),
             in_=wq_raw_sc[:].rearrange("p (m t) -> p t m", t=PACK),
@@ -102,16 +94,26 @@ def tile_attend_passedtwo_madeparts_kernel(
         nc.vector.quantize_mx(
             out=st_w[:].bitcast(FP8X4), scales=st_sc[:], in_=st_bf[:].rearrange("p q j -> p (q j)")
         )
-
+        pairs = [slice(0, 2), slice(2, 4)]
         qv_ps = ps.tile([P, PACK, Q], F32)
-        for t in range(PACK):
-            cols = slice(t * P, (t + 1) * P)
-            nc.tensor.matmul_mx(
-                out=qv_ps[:, t, :],
-                lhsT=wq_w[:, cols].bitcast(FP8X4), lhsT_scale=wq_sc[:, cols],
-                rhs=st_w[:].bitcast(FP8X4), rhs_scale=st_sc[:],
-                start=True, stop=True,
+        for u, pair in enumerate(pairs):
+            deal = nc.vector.tensor_copy if u == 0 else nc.scalar.copy
+            deal(
+                out=wq_w[:].rearrange("p (t m) -> p m t", t=PACK)[:, :, pair],
+                in_=wq_raw[:].rearrange("p (m t) -> p m t", t=PACK)[:, :, pair],
             )
+            for e in range(2):
+                cols = slice((2 * u + e) * P, (2 * u + e + 1) * P)
+                nc.tensor.matmul_mx(
+                    out=qv_ps[:, 2 * u + e, :],
+                    lhsT=wq_w[:, cols].bitcast(FP8X4), lhsT_scale=wq_sc[:, cols],
+                    rhs=st_w[:].bitcast(FP8X4), rhs_scale=st_sc[:],
+                    start=True, stop=True,
+                )
+        f1 = sb.tile([P, T], F32, align_bytes=64)
+        f2 = sb.tile([P, T], F32, align_bytes=64)
+        nc.vector.memset(f1[:], 0.0)
+        nc.vector.memset(f2[:], 0.0)
         banks = [ps.tile([P, N_SCORE], F32, name="score%d" % b) for b in range(T // N_SCORE)]
         for b, bank in enumerate(banks):
             cols = slice(b * N_SCORE, (b + 1) * N_SCORE)

from contextlib import ExitStack

import concourse.mybir as mybir

D, K, T, I, Q = 512, 512, 1024, 512, 128
FLOPS = 2 * Q * (D * K + K * T + D * T)

F32 = mybir.dt.float32
BF16 = mybir.dt.bfloat16
I32 = mybir.dt.int32
U32 = mybir.dt.uint32
U16 = mybir.dt.uint16
U8 = mybir.dt.uint8
FP8X4 = mybir.dt.float8_e4m3fn_x4
FP4X4 = mybir.dt.float4_e2m1fn_x4
COPY = mybir.ActivationFunctionType.Copy
ALU = mybir.AluOpType

P = 128
PACK = 4
N_SCORE = 256
HALF = I // 2
COLS = HALF // 16


def load_scales_all(queue, plane, rows):
    for quad in range(4):
        src = rows[0, 4 * quad : 4 * quad + 4, :].bitcast(I32)
        queue.dma_start(
            out=plane[32 * quad : 32 * quad + 32, :].bitcast(I32),
            in_=src.unsqueeze(0).to_broadcast([8, 4, src.shape[1]]),
        )


def load_scales(queue, plane, rows, quads=range(4)):
    for quad in quads:
        queue.dma_start(
            out=plane[32 * quad : 32 * quad + 4, :].bitcast(I32),
            in_=rows[0, 4 * quad : 4 * quad + 4, :].bitcast(I32),
        )


def tile_attend_passedtwo_madeparts_kernel(
    tc, states, wq_words, wq_scales, keys_words, keys_scales, tags_words, tags_scales,
    offs, offs2, offs3, offs4, offs5, offs6, out,
):
    nc = tc.nc
    with ExitStack() as ctx:
        sb = ctx.enter_context(tc.tile_pool(name="sb", bufs=1))
        ps = ctx.enter_context(tc.psum_pool(name="ps", bufs=1))

        lists = [sb.tile([P, I // 16], U16, name="list%d" % n) for n in range(6)]
        wq_raw_sc = sb.tile([P, K], U8, align_bytes=64)
        keys_sc = sb.tile([P, T], U8, align_bytes=64)
        tags_sc = sb.tile([P, T], U8, align_bytes=64)
        st_raw = sb.tile([P, PACK, Q], F32, align_bytes=64)
        wq_raw = sb.tile([P, K], U32, align_bytes=64)
        keys_w = sb.tile([P, 2 * T], U8, align_bytes=64)
        tags_w = sb.tile([P, T], U32, align_bytes=64)


        nc.sync.dma_start(out=st_raw[:], in_=states.rearrange("(p j) q -> p j q", j=PACK))
        load_scales_all(nc.sync, wq_raw_sc, wq_scales)
        nc.sync.dma_start(
            out=wq_raw[:].bitcast(I32), in_=wq_words[0].rearrange("p n t -> p (n t)").bitcast(I32)
        )
        load_scales(nc.gpsimd, keys_sc, keys_scales, (3,))
        load_scales(nc.sync, tags_sc, tags_scales, (0,))
        nc.sync.dma_start(
            out=tags_w[:].bitcast(I32), in_=tags_words[0].rearrange("p n t -> p (n t)").bitcast(I32)
        )
        load_scales(nc.sync, tags_sc, tags_scales, (1, 2, 3))
        nc.sync.dma_start(out=keys_w[:].bitcast(I32), in_=keys_words[0].bitcast(I32))
        load_scales(nc.sync, keys_sc, keys_scales, (0, 1, 2))
        for tile, src in zip(lists, (offs, offs2, offs3, offs4, offs5, offs6)):
            nc.sync.dma_start(tile[:], src)


        st_bf = sb.tile([P, Q, PACK], BF16, align_bytes=64)
        nc.scalar.activation(
            st_bf[:, Q // 2 :, :], st_raw[:, :, Q // 2 :].rearrange("p j q -> p q j"), COPY
        )
        nc.vector.tensor_copy(
            out=st_bf[:, : Q // 2, :], in_=st_raw[:, :, : Q // 2].rearrange("p j q -> p q j")
        )
        wq_w = sb.tile([P, K], U32, align_bytes=64)
        wq_sc = sb.tile([P, K], U8, align_bytes=64)
        nc.vector.tensor_copy(
            out=wq_sc[:].rearrange("p (t m) -> p t m", t=PACK),
            in_=wq_raw_sc[:].rearrange("p (m t) -> p t m", t=PACK),
        )
        st_w = sb.tile([P, Q], U32, align_bytes=64)
        st_sc = sb.tile([P, Q], U8, align_bytes=64)
        nc.vector.quantize_mx(
            out=st_w[:].bitcast(FP8X4), scales=st_sc[:], in_=st_bf[:].rearrange("p q j -> p (q j)")
        )
        pairs = [slice(0, 2), slice(2, 4)]
        qv_ps = ps.tile([P, PACK, Q], F32)
        for u, pair in enumerate(pairs):
            deal = nc.vector.tensor_copy if u == 0 else nc.scalar.copy
            deal(
                out=wq_w[:].rearrange("p (t m) -> p m t", t=PACK)[:, :, pair],
                in_=wq_raw[:].rearrange("p (m t) -> p m t", t=PACK)[:, :, pair],
            )
            for e in range(2):
                cols = slice((2 * u + e) * P, (2 * u + e + 1) * P)
                nc.tensor.matmul_mx(
                    out=qv_ps[:, 2 * u + e, :],
                    lhsT=wq_w[:, cols].bitcast(FP8X4), lhsT_scale=wq_sc[:, cols],
                    rhs=st_w[:].bitcast(FP8X4), rhs_scale=st_sc[:],
                    start=True, stop=True,
                )
        f1 = sb.tile([P, T], F32, align_bytes=64)
        f2 = sb.tile([P, T], F32, align_bytes=64)
        nc.vector.memset(f1[:], 0.0)
        nc.vector.memset(f2[:], 0.0)
        banks = [ps.tile([P, N_SCORE], F32, name="score%d" % b) for b in range(T // N_SCORE)]
        for b, bank in enumerate(banks):
            cols = slice(b * N_SCORE, (b + 1) * N_SCORE)
            nc.tensor.matmul_mx(
                out=bank[:],
                lhsT=st_w[:].bitcast(FP8X4), lhsT_scale=st_sc[:],
                rhs=tags_w[:, cols].bitcast(FP8X4), rhs_scale=tags_sc[:, cols],
                start=True, stop=False,
            )

        qv_bf = sb.tile([P, Q, PACK], BF16, align_bytes=64)
        nc.scalar.copy(out=qv_bf[:], in_=qv_ps[:].rearrange("p t q -> p q t"))
        qv_w = sb.tile([P, Q], U32, align_bytes=64)
        qv_sc = sb.tile([P, Q], U8, align_bytes=64)
        nc.vector.quantize_mx(
            out=qv_w[:].bitcast(FP8X4), scales=qv_sc[:], in_=qv_bf[:].rearrange("p q t -> p (q t)")
        )

        a = sb.tile([P, T], F32, align_bytes=64)
        for b, bank in enumerate(banks):
            cols = slice(b * N_SCORE, (b + 1) * N_SCORE)
            nc.tensor.matmul_mx(
                out=bank[:],
                lhsT=qv_w[:].bitcast(FP8X4), lhsT_scale=qv_sc[:],
                rhs=keys_w[:, 2 * cols.start : 2 * cols.stop].bitcast(FP4X4), rhs_scale=keys_sc[:, cols],
                start=False, stop=True,
            )
            if b % 2 == 0:
                nc.scalar.copy(out=a[:, cols], in_=bank[:])
            else:
                nc.vector.tensor_copy(out=a[:, cols], in_=bank[:])

        g1 = sb.tile([P, I], F32, align_bytes=64)
        g2 = sb.tile([P, I], F32, align_bytes=64)
        nc.vector.tensor_copy(g1[:, :HALF], a[:].indirect(lists[0][:, :COLS]))
        nc.scalar.activation(g1[:, HALF:], a[:].indirect(lists[0][:, COLS:]), COPY)
        nc.scalar.activation(g2[:], a[:].indirect(lists[1][:]), COPY)
        nc.vector.tensor_copy(f1[:].indirect(lists[2][:]), g1[:])
        nc.vector.tensor_copy(f2[:].indirect(lists[3][:]), g2[:])

        r = sb.tile([P, T], F32, align_bytes=64)
        cc = sb.tile([P, T], F32, align_bytes=64)
        halves = [slice(h * T // 2, (h + 1) * T // 2) for h in range(2)]
        for cols in halves:
            nc.vector.tensor_tensor(r[:, cols], f1[:, cols], f2[:, cols], ALU.max)
        for cols in halves:
            nc.vector.tensor_tensor(cc[:, cols], r[:, cols], a[:, cols], ALU.add)

        y5 = sb.tile([P, I], F32, align_bytes=64)
        y6 = sb.tile([P, I], F32, align_bytes=64)
        y = sb.tile([P, I], F32, align_bytes=64)
        for h in range(2):
            cols = slice(h * HALF, (h + 1) * HALF)
            lc = slice(h * COLS, (h + 1) * COLS)
            nc.vector.tensor_copy(y5[:, cols], cc[:].indirect(lists[4][:, lc]))
            nc.scalar.activation(y6[:, cols], cc[:].indirect(lists[5][:, lc]), COPY)
        for h in range(2):
            cols = slice(h * HALF, (h + 1) * HALF)
            nc.vector.tensor_tensor(y[:, cols], y5[:, cols], y6[:, cols], ALU.subtract)
            nc.sync.dma_start(out=out[:, cols], in_=y[:, cols])
